import numpy as np
import ml_dtypes


def mxq(x, axis, fmt="e4m3"):
    dtype, down = {"e4m3": (ml_dtypes.float8_e4m3fn, 7), "e5m2": (ml_dtypes.float8_e5m2, 14)}[fmt]
    v = np.moveaxis(np.asarray(x, np.float32).astype(ml_dtypes.bfloat16).astype(np.float64), axis, -1)
    blocks = v.reshape(v.shape[:-1] + (-1, 32))
    amax = np.abs(blocks).max(-1, keepdims=True)
    byte = np.maximum(np.where(amax > 0, np.frexp(amax)[1] - 1 + 127, 0) - down, 1)
    scale = np.exp2(byte - 127.0)
    codes = (blocks / scale).astype(np.float32).astype(dtype).astype(np.float64)
    return np.moveaxis((codes * scale).reshape(v.shape), -1, axis)


WIDE = False


def mx_kscale(k, group=512):
    if not WIDE:
        return np.ones(k)
    levels = np.array([18, -18])
    if group != 512:
        return np.exp2(np.random.permutation(np.resize(levels, k // group))).repeat(group)
    if k % 512:
        return np.exp2(np.random.permutation(np.resize(levels, k // 32))).repeat(32)
    a = np.empty((k // 512, 16))
    for p in range(k // 512):
        a[p, :8] = np.random.permutation(np.resize(levels, 8))
        for g in range(8):
            far = levels[np.abs(levels - a[p, g]) >= 10]
            a[p, g + 8] = far[np.random.randint(len(far))]
    return np.exp2(a.ravel()).repeat(32)


def f64(x):
    return np.asarray(x).astype(np.float64)


G, D, M, N = 4, 128, 128, 512


def setup_inputs():
    n = np.random.standard_normal
    s_d = mx_kscale(D, 0)
    return {
        "dy": (n((G, D, N)) * s_d[:, None]).astype(np.float32),
        "w": (n((G, D, M)) / np.sqrt(D) / s_d[:, None]).astype(np.float32),
        "th": (np.tanh(n((G, M, N)))).astype(np.float32),
    }


def reference(dy, w, th):
    wq = mxq(f64(w), 1, "e5m2")
    dyq = mxq(f64(dy), 1, "e5m2")
    z = wq.transpose(0, 2, 1) @ dyq
    y = z * (1.0 - np.square(f64(th)))
    return y

@@ -1,0 +1,103 @@
+from contextlib import ExitStack
+
+import concourse.mybir as mybir
+
+G, D, M, N = 4, 128, 128, 512
+FLOPS = 2 * G * D * M * N
+
+F32 = mybir.dt.float32
+BF16 = mybir.dt.bfloat16
+U32 = mybir.dt.uint32
+U8 = mybir.dt.uint8
+E5M2X4 = mybir.dt.float8_e5m2_x4
+ALU = mybir.AluOpType
+ACT = mybir.ActivationFunctionType
+
+P = 128
+PACK = 4
+ROWS = D // PACK
+RUN = 4
+HALF = N // 2
+DY_VECTOR = 160
+W_VECTOR = 88
+
+
+def views(raw, grouped, c0, c1):
+    src = raw[:, :, c0:c1].rearrange("p j (c i) -> p c j i", i=RUN)
+    dst = grouped[:, c0:c1, :].rearrange("p (c i) j -> p c j i", i=RUN)
+    return dst, src
+
+
+def tile_rows_gback_tanh_kernel(tc, dy, w, th, out):
+    nc = tc.nc
+    dy_rows = dy.rearrange("g (p j) n -> (g p) j n", j=PACK)
+    w_rows = w.rearrange("g (p j) m -> (g p) j m", j=PACK)
+
+    with ExitStack() as ctx:
+        sb = ctx.enter_context(tc.tile_pool(name="sb", bufs=1))
+        ps = ctx.enter_context(tc.psum_pool(name="ps", bufs=1))
+        ctx.enter_context(tc.manual_schedule())
+
+        dy_raw = [sb.tile([P, PACK, HALF], F32, name="dy_raw%d" % h, align_bytes=64) for h in range(2)]
+        w_raw = sb.tile([P, PACK, M], F32, align_bytes=64)
+        th_raw = [sb.tile([M, N], F32, name="th_raw%d" % g, align_bytes=64) for g in range(G)]
+        th_sq = [sb.tile([M, N], F32, name="th_sq%d" % g, align_bytes=64) for g in range(G)]
+        res = [sb.tile([M, N], F32, name="res%d" % g, align_bytes=64) for g in range(G)]
+        dy_bf = [sb.tile([P, HALF, PACK], BF16, name="dy_bf%d" % h, align_bytes=64) for h in range(2)]
+        w_bf = sb.tile([P, M, PACK], BF16, align_bytes=64)
+        dy_codes = sb.tile([P, N], U32, align_bytes=64)
+        dy_scales = sb.tile([P, N], U8, align_bytes=64)
+        w_codes = sb.tile([P, M], U32, align_bytes=64)
+        w_scales = sb.tile([P, M], U8, align_bytes=64)
+        warm_in = sb.tile([P, 8], F32, align_bytes=64)
+        warm_out = sb.tile([P, 8], F32, align_bytes=64)
+        acc = [ps.tile([M, N], F32, name="acc%d" % g) for g in range(G)]
+
+        for h in range(2):
+            nc.sync.dma_start(out=dy_raw[h][:], in_=dy_rows[:, :, h * HALF : (h + 1) * HALF])
+        nc.sync.dma_start(out=w_raw[:], in_=w_rows)
+        for g in range(G):
+            nc.sync.dma_start(out=th_raw[g][:], in_=th[g])
+
+        nc.vector.memset(warm_in[:], 0.0)
+        nc.scalar.activation(out=warm_out[:], in_=warm_in[:], func=ACT.Square)
+
+        def interleave_dy(h):
+            dst, src = views(dy_raw[h], dy_bf[h], 0, DY_VECTOR)
+            nc.vector.tensor_copy(out=dst, in_=src)
+            dst, src = views(dy_raw[h], dy_bf[h], DY_VECTOR, HALF)
+            nc.scalar.copy(out=dst, in_=src)
+
+        def quantize(codes, scales, grouped):
+            nc.vector.quantize_mx(
+                out=codes.bitcast(E5M2X4), scales=scales, in_=grouped[:].rearrange("p c j -> p (c j)")
+            )
+
+        interleave_dy(0)
+        quantize(dy_codes[:, 0:HALF], dy_scales[:, 0:HALF], dy_bf[0])
+        interleave_dy(1)
+        dst, src = views(w_raw, w_bf, 0, W_VECTOR)
+        nc.vector.tensor_scalar(out=dst, in0=src, scalar1=-1.0, scalar2=None, op0=ALU.mult)
+        dst, src = views(w_raw, w_bf, W_VECTOR, M)
+        nc.scalar.activation(out=dst, in_=src, func=ACT.Copy, scale=-1.0)
+        quantize(dy_codes[:, HALF:N], dy_scales[:, HALF:N], dy_bf[1])
+        quantize(w_codes[:], w_scales[:], w_bf)
+
+        for g in range(G):
+            rows = slice(g * ROWS, (g + 1) * ROWS)
+            nc.tensor.matmul_mx(
+                out=acc[g][:],
+                lhsT=w_codes[rows, :].bitcast(E5M2X4),
+                lhsT_scale=w_scales[rows, :],
+                rhs=dy_codes[rows, :].bitcast(E5M2X4),
+                rhs_scale=dy_scales[rows, :],
+                start=True,
+                stop=True,
+            )
+
+        for g in range(G):
+            nc.scalar.activation(out=th_sq[g][:], in_=th_raw[g][:], func=ACT.Square)
+            nc.vector.scalar_tensor_tensor(
+                out=res[g][:], in0=th_sq[g][:], scalar=1.0, in1=acc[g][:], op0=ALU.subtract, op1=ALU.mult
+            )
+            nc.sync.dma_start(out=out[g], in_=res[g][:])

@@ -51,6 +51,10 @@ def tile_rows_gback_tanh_kernel(tc, dy, w, th, out):
         w_scales = sb.tile([P, M], U8, align_bytes=64)
         warm_in = sb.tile([P, 8], F32, align_bytes=64)
         warm_out = sb.tile([P, 8], F32, align_bytes=64)
+        zero_bf = sb.tile([P, M, PACK], BF16, align_bytes=64)
+        zero_codes = sb.tile([P, N], U32, align_bytes=64)
+        zero_scales = sb.tile([P, N], U8, align_bytes=64)
+        idle = [ps.tile([M, N], F32, name="idle%d" % g) for g in range(G)]
         acc = [ps.tile([M, N], F32, name="acc%d" % g) for g in range(G)]
 
         for h in range(2):
@@ -70,30 +74,41 @@ def tile_rows_gback_tanh_kernel(tc, dy, w, th, out):
 
         def quantize(codes, scales, grouped):
             nc.vector.quantize_mx(
-                out=codes.bitcast(E5M2X4), scales=scales, in_=grouped[:].rearrange("p c j -> p (c j)")
+                out=codes.bitcast(E5M2X4), scales=scales, in_=grouped.rearrange("p c j -> p (c j)")
             )
 
+        def multiply(banks, lhs_codes, lhs_scales, rhs_codes, rhs_scales):
+            for g in range(G):
+                rows = slice(g * ROWS, (g + 1) * ROWS)
+                nc.tensor.matmul_mx(
+                    out=banks[g][:],
+                    lhsT=lhs_codes[rows, 0:M].bitcast(E5M2X4),
+                    lhsT_scale=lhs_scales[rows, 0:M],
+                    rhs=rhs_codes[rows, :].bitcast(E5M2X4),
+                    rhs_scale=rhs_scales[rows, :],
+                    start=True,
+                    stop=True,
+                )
+
+        nc.vector.memset(zero_bf[:].rearrange("p c j -> p (c j)").bitcast(U32), 0)
+        for c0 in range(0, N, M):
+            quantize(zero_codes[:, c0 : c0 + M], zero_scales[:, c0 : c0 + M], zero_bf[:])
+        for r in range(3):
+            multiply(idle, zero_codes, zero_scales, zero_codes, zero_scales)
+
         interleave_dy(0)
-        quantize(dy_codes[:, 0:HALF], dy_scales[:, 0:HALF], dy_bf[0])
+        quantize(dy_codes[:, 0:HALF], dy_scales[:, 0:HALF], dy_bf[0][:])
+        for r in range(2):
+            multiply(idle, dy_codes, dy_scales, zero_codes, zero_scales)
         interleave_dy(1)
         dst, src = views(w_raw, w_bf, 0, W_VECTOR)
         nc.vector.tensor_scalar(out=dst, in0=src, scalar1=-1.0, scalar2=None, op0=ALU.mult)
         dst, src = views(w_raw, w_bf, W_VECTOR, M)
         nc.scalar.activation(out=dst, in_=src, func=ACT.Copy, scale=-1.0)
-        quantize(dy_codes[:, HALF:N], dy_scales[:, HALF:N], dy_bf[1])
-        quantize(w_codes[:], w_scales[:], w_bf)
+        quantize(dy_codes[:, HALF:N], dy_scales[:, HALF:N], dy_bf[1][:])
+        quantize(w_codes[:], w_scales[:], w_bf[:])
 
-        for g in range(G):
-            rows = slice(g * ROWS, (g + 1) * ROWS)
-            nc.tensor.matmul_mx(
-                out=acc[g][:],
-                lhsT=w_codes[rows, :].bitcast(E5M2X4),
-                lhsT_scale=w_scales[rows, :],
-                rhs=dy_codes[rows, :].bitcast(E5M2X4),
-                rhs_scale=dy_scales[rows, :],
-                start=True,
-                stop=True,
-            )
+        multiply(acc, w_codes, w_scales, dy_codes, dy_scales)
 
         for g in range(G):
             nc.scalar.activation(out=th_sq[g][:], in_=th_raw[g][:], func=ACT.Square)

@@ -19,7 +19,7 @@ ROWS = D // PACK
 RUN = 4
 HALF = N // 2
 DY_VECTOR = 160
-W_VECTOR = 88
+W_VECTOR = 72
 
 
 def views(raw, grouped, c0, c1):
@@ -93,7 +93,7 @@ def tile_rows_gback_tanh_kernel(tc, dy, w, th, out):
         nc.vector.memset(zero_bf[:].rearrange("p c j -> p (c j)").bitcast(U32), 0)
         for c0 in range(0, N, M):
             quantize(zero_codes[:, c0 : c0 + M], zero_scales[:, c0 : c0 + M], zero_bf[:])
-        for r in range(3):
+        for r in range(4):
             multiply(idle, zero_codes, zero_scales, zero_codes, zero_scales)
 
         interleave_dy(0)

from contextlib import ExitStack

import concourse.mybir as mybir

G, D, M, N = 4, 128, 128, 512
FLOPS = 2 * G * D * M * N

F32 = mybir.dt.float32
BF16 = mybir.dt.bfloat16
U32 = mybir.dt.uint32
U8 = mybir.dt.uint8
E5M2X4 = mybir.dt.float8_e5m2_x4
ALU = mybir.AluOpType
ACT = mybir.ActivationFunctionType

P = 128
PACK = 4
ROWS = D // PACK
RUN = 4
HALF = N // 2
DY_VECTOR = 160
W_VECTOR = 72


def views(raw, grouped, c0, c1):
    src = raw[:, :, c0:c1].rearrange("p j (c i) -> p c j i", i=RUN)
    dst = grouped[:, c0:c1, :].rearrange("p (c i) j -> p c j i", i=RUN)
    return dst, src


def tile_rows_gback_tanh_kernel(tc, dy, w, th, out):
    nc = tc.nc
    dy_rows = dy.rearrange("g (p j) n -> (g p) j n", j=PACK)
    w_rows = w.rearrange("g (p j) m -> (g p) j m", j=PACK)

    with ExitStack() as ctx:
        sb = ctx.enter_context(tc.tile_pool(name="sb", bufs=1))
        ps = ctx.enter_context(tc.psum_pool(name="ps", bufs=1))
        ctx.enter_context(tc.manual_schedule())

        dy_raw = [sb.tile([P, PACK, HALF], F32, name="dy_raw%d" % h, align_bytes=64) for h in range(2)]
        w_raw = sb.tile([P, PACK, M], F32, align_bytes=64)
        th_raw = [sb.tile([M, N], F32, name="th_raw%d" % g, align_bytes=64) for g in range(G)]
        th_sq = [sb.tile([M, N], F32, name="th_sq%d" % g, align_bytes=64) for g in range(G)]
        res = [sb.tile([M, N], F32, name="res%d" % g, align_bytes=64) for g in range(G)]
        dy_bf = [sb.tile([P, HALF, PACK], BF16, name="dy_bf%d" % h, align_bytes=64) for h in range(2)]
        w_bf = sb.tile([P, M, PACK], BF16, align_bytes=64)
        dy_codes = sb.tile([P, N], U32, align_bytes=64)
        dy_scales = sb.tile([P, N], U8, align_bytes=64)
        w_codes = sb.tile([P, M], U32, align_bytes=64)
        w_scales = sb.tile([P, M], U8, align_bytes=64)
        warm_in = sb.tile([P, 8], F32, align_bytes=64)
        warm_out = sb.tile([P, 8], F32, align_bytes=64)
        zero_bf = sb.tile([P, M, PACK], BF16, align_bytes=64)
        zero_codes = sb.tile([P, N], U32, align_bytes=64)
        zero_scales = sb.tile([P, N], U8, align_bytes=64)
        idle = [ps.tile([M, N], F32, name="idle%d" % g) for g in range(G)]
        acc = [ps.tile([M, N], F32, name="acc%d" % g) for g in range(G)]

        for h in range(2):
            nc.sync.dma_start(out=dy_raw[h][:], in_=dy_rows[:, :, h * HALF : (h + 1) * HALF])
        nc.sync.dma_start(out=w_raw[:], in_=w_rows)
        for g in range(G):
            nc.sync.dma_start(out=th_raw[g][:], in_=th[g])

        nc.vector.memset(warm_in[:], 0.0)
        nc.scalar.activation(out=warm_out[:], in_=warm_in[:], func=ACT.Square)

        def interleave_dy(h):
            dst, src = views(dy_raw[h], dy_bf[h], 0, DY_VECTOR)
            nc.vector.tensor_copy(out=dst, in_=src)
            dst, src = views(dy_raw[h], dy_bf[h], DY_VECTOR, HALF)
            nc.scalar.copy(out=dst, in_=src)

        def quantize(codes, scales, grouped):
            nc.vector.quantize_mx(
                out=codes.bitcast(E5M2X4), scales=scales, in_=grouped.rearrange("p c j -> p (c j)")
            )

        def multiply(banks, lhs_codes, lhs_scales, rhs_codes, rhs_scales):
            for g in range(G):
                rows = slice(g * ROWS, (g + 1) * ROWS)
                nc.tensor.matmul_mx(
                    out=banks[g][:],
                    lhsT=lhs_codes[rows, 0:M].bitcast(E5M2X4),
                    lhsT_scale=lhs_scales[rows, 0:M],
                    rhs=rhs_codes[rows, :].bitcast(E5M2X4),
                    rhs_scale=rhs_scales[rows, :],
                    start=True,
                    stop=True,
                )

        nc.vector.memset(zero_bf[:].rearrange("p c j -> p (c j)").bitcast(U32), 0)
        for c0 in range(0, N, M):
            quantize(zero_codes[:, c0 : c0 + M], zero_scales[:, c0 : c0 + M], zero_bf[:])
        for r in range(4):
            multiply(idle, zero_codes, zero_scales, zero_codes, zero_scales)

        interleave_dy(0)
        quantize(dy_codes[:, 0:HALF], dy_scales[:, 0:HALF], dy_bf[0][:])
        for r in range(2):
            multiply(idle, dy_codes, dy_scales, zero_codes, zero_scales)
        interleave_dy(1)
        dst, src = views(w_raw, w_bf, 0, W_VECTOR)
        nc.vector.tensor_scalar(out=dst, in0=src, scalar1=-1.0, scalar2=None, op0=ALU.mult)
        dst, src = views(w_raw, w_bf, W_VECTOR, M)
        nc.scalar.activation(out=dst, in_=src, func=ACT.Copy, scale=-1.0)
        quantize(dy_codes[:, HALF:N], dy_scales[:, HALF:N], dy_bf[1][:])
        quantize(w_codes[:], w_scales[:], w_bf[:])

        multiply(acc, w_codes, w_scales, dy_codes, dy_scales)

        for g in range(G):
            nc.scalar.activation(out=th_sq[g][:], in_=th_raw[g][:], func=ACT.Square)
            nc.vector.scalar_tensor_tensor(
                out=res[g][:], in0=th_sq[g][:], scalar=1.0, in1=acc[g][:], op0=ALU.subtract, op1=ALU.mult
            )
            nc.sync.dma_start(out=out[g], in_=res[g][:])
